import numpy as np, ml_dtypes
CORES = [24,25,26,27,28,29,30,31,224,225,226,227,228,229,230,231]
N = 16
F = 512
def setup_inputs(rng):
    m = (rng.standard_normal((N, 128, 128), dtype=np.float32) / 11).astype(ml_dtypes.bfloat16)
    return {"m": m, "mt": m.transpose(0, 2, 1).copy(), "x": rng.standard_normal((N, 128, F), dtype=np.float32).astype(ml_dtypes.bfloat16)}
def setup_inputs_big(rng):
    d = setup_inputs(rng)
    for k in ("x",): d[k] = (d[k].astype(np.float32) * 1048576.0).astype(d[k].dtype)
    return d
def setup_inputs_small(rng):
    d = setup_inputs(rng)
    for k in ("x",): d[k] = (d[k].astype(np.float32) * (1 / 1048576.0)).astype(d[k].dtype)
    return d
def setup_inputs_apart(rng):
    d = setup_inputs(rng)
    f = (10.0 ** rng.permutation(np.linspace(-1.5, 1.5, N))).astype(np.float32).reshape(N, 1, 1)
    for k in ("x",): d[k] = (d[k].astype(np.float32) * f).astype(d[k].dtype)
    return d
def reference(m, mt, x):
    M, X = m.astype(np.float64), x.astype(np.float64)
    y = np.zeros((N, 128, F)); p = X[0]
    for r in range(N):
        p = M[r].T @ p
        y[r] = p
    return {"y": y.astype(ml_dtypes.bfloat16)}

@@ -1,0 +1,314 @@
+from concourse.bass import DstId, RemoteDMATransfer
+
+P = 128
+F = 512
+NBANK = 8
+NSLOT = 10
+NPROD = 14
+
+SCRATCH = {
+    "xin": ("sbuf", [P, F], "bfloat16"),
+    "lf": ("sbuf", [P, 8 * P], "bfloat16"),
+    "own2": ("sbuf", [P, P], "bfloat16"),
+    "hp": ("sbuf", [P, P], "bfloat16"),
+    "prod": ("sbuf", [P, NSLOT * P], "bfloat16"),
+    "pl": ("sbuf", [P, F], "bfloat16"),
+    "pf": ("sbuf", [P, F], "bfloat16"),
+    "yout": ("sbuf", [P, F], "bfloat16"),
+}
+for _b in range(NBANK):
+    SCRATCH["ps%d" % _b] = ("psum", [P, 512], "float32")
+
+SEMAPHORES = (["lda", "ldb", "ldx", "pf", "hp", "sent"] + ["lf%d" % i for i in range(8)] + ["pq%d" % i for i in range(4)]
+              + ["st%d" % i for i in range(4)] + ["t%d" % i for i in range(NPROD)] + ["v%d" % i for i in range(NPROD)])
+
+
+def bits(m):
+    return bin(m).count("1")
+
+
+def share(m, k, n):
+    es = [e for e in range(m.bit_length()) if (m >> e) & 1]
+    out = 0
+    for e in es[k::n]:
+        out |= 1 << e
+    return out
+
+
+def split(a, b):
+    k = b.bit_length()
+    while True:
+        t = (b >> k) << k
+        if t > a:
+            return t
+        k -= 1
+
+
+def expand(node, given, nodes, leaves):
+    a, b, tr = node
+    if node in given or node in nodes or node in leaves:
+        return
+    if a == b:
+        leaves.append(node)
+        return
+    t = split(a, b)
+    expand((a, t - 1, True), given, nodes, leaves)
+    expand((t, b, False), given, nodes, leaves)
+    nodes.append(node)
+
+
+def height(node, given):
+    a, b, tr = node
+    if a == b or node in given:
+        return 0
+    t = split(a, b)
+    return 1 + max(height((a, t - 1, True), given), height((t, b, False), given))
+
+
+def layout(cores, topo):
+    root = cores[0]
+    rk = {}
+    for i, c in enumerate(cores):
+        rk[c] = i
+
+    def place(c):
+        return (topo.host(c), topo.chip(c))
+
+    def neighbours(c, chipcores):
+        return [d for d in chipcores if d != c and topo.die(d) == topo.die(c)]
+
+    A = [c for c in cores if place(c) == place(root)]
+    B = [c for c in cores if place(c) != place(root)]
+    relays = [c for c in A if c != root and topo.may_write(c, B[0])]
+    nq = len(relays)
+    w = F // nq
+    home = neighbours(root, A)
+    far = [c for c in A if topo.die(c) != topo.die(root)]
+    piece = {}
+    for q, c in enumerate(relays):
+        piece[c] = q
+    spare = [q for q, c in enumerate(relays) if c not in far]
+    for c in far:
+        if c not in piece:
+            piece[c] = spare.pop(0)
+    b1 = [c for c in B if topo.die(c) == topo.die(B[0])]
+    b2 = [c for c in B if topo.die(c) != topo.die(B[0])]
+    for grp in (b1, b2):
+        for k, c in enumerate(grp):
+            piece[c] = k
+    helper = B[-1]
+    shared = (rk[b1[0]], rk[b1[-1]], True)
+    first = {}
+    for c in A:
+        first[c] = rk[A[1]]
+    for c in B:
+        first[c] = rk[B[0]]
+
+    def given_away(c):
+        j = rk[c]
+        return (j, j, j % 2 == 0 or j == first[c])
+
+    work = {}
+    for c in cores[1:]:
+        given = [shared] if (c in b2 and c != helper) else []
+        urgent = [(first[c], rk[A[-1]], False)] if c in relays else ([shared] if c == helper else [])
+        final = (first[c], rk[c], False)
+        n1, n2, leaves = [], [], []
+        for nd in urgent:
+            expand(nd, given, n1, leaves)
+        n2 = list(n1)
+        expand(final, given, n2, leaves)
+        n2 = n2[len(n1):]
+        n1.sort(key=lambda nd: height(nd, given))
+        n2.sort(key=lambda nd: height(nd, given))
+        work[c] = (n1, n2, leaves, given, final, urgent)
+
+    calls = {}
+
+    def add(src, label, dsts, mask, sem, buf, c0, c1):
+        if dsts:
+            calls.setdefault((src, label), []).append((dsts, mask, sem, buf, c0, c1))
+
+    hr = [c for c in relays if c in home]
+    fr = [c for c in relays if c in far]
+    order = []
+    for i in range(max(len(hr), len(fr))):
+        order += hr[i:i + 1] + fr[i:i + 1]
+    for k, c in enumerate(order):
+        q = piece[c]
+        add(root, "scatter", [c], share(topo.mask(root, c), k, len(order)), "pq%d" % q, "pl", q * w, (q + 1) * w)
+    rest = [c for c in far if c not in relays]
+    for k, c in enumerate(rest):
+        q = piece[c]
+        add(root, "scatter2", [c], share(topo.mask(root, c), k, len(rest)), "pq%d" % q, "pl", q * w, (q + 1) * w)
+    add(root, "full", home, topo.mask(root, home[0]), "pf", "pf", 0, F)
+    slot = {}
+    for chipcores, prio in ((A, relays), (B, [helper])):
+        for s, src in enumerate(chipcores):
+            slot[src] = s
+            if src == root:
+                continue
+            need = [c for c in chipcores if c != src and c != root and given_away(src) in work[c][2]]
+            for label, dsts in (("leaf1", [c for c in need if c in prio]), ("leaf2", [c for c in need if c not in prio])):
+                if dsts:
+                    add(src, label, dsts, topo.mask(src, dsts[0]), "lf%d" % s, "lf", s * P, (s + 1) * P)
+    for c in relays:
+        q = piece[c]
+        dsts = [d for d in B if piece[d] == q]
+        add(c, "p7", dsts, topo.mask(c, dsts[0]), "pq%d" % q, "pl", q * w, (q + 1) * w)
+    for chipcores, holders in ((A, far), (B, B)):
+        for c in holders:
+            q = piece[c]
+            dsts = neighbours(c, chipcores)
+            add(c, "fwd", dsts, topo.mask(c, dsts[0]), "pq%d" % q, "pl", q * w, (q + 1) * w)
+    dsts = [c for c in b2 if c != helper]
+    add(helper, "node", dsts, topo.mask(helper, dsts[0]), "hp", "hp", 0, P)
+
+    expect = {}
+    for key in calls:
+        for (dsts, mask, sem, buf, c0, c1) in calls[key]:
+            for d in dsts:
+                expect[(d, sem)] = expect.get((d, sem), 0) + bits(mask)
+    return dict(root=root, rk=rk, A=A, B=B, relays=relays, nq=nq, w=w, home=home, far=far, piece=piece, helper=helper,
+                shared=shared, work=work, calls=calls, expect=expect, slot=slot, given_away=given_away)
+
+
+def rank_program(g, core, T, topo):
+    rank = T.rank_of(core)
+    if rank is None:
+        return
+    L = layout(list(T.cores), topo)
+    nq, w, calls, expect = L["nq"], L["w"], L["calls"], L["expect"]
+    incs = {}
+    waited = set()
+    tdone = set()
+    count = [0, 0]
+
+    for (d, sem) in expect:
+        if d == core:
+            incs[sem] = expect[(d, sem)]
+
+    def wait(queue, sem):
+        queue.wait_ge(T.sem[sem], incs[sem])
+        waited.add(sem)
+
+    def twait(sem):
+        if sem not in tdone:
+            tdone.add(sem)
+            wait(g.tensor, sem)
+
+    def load(queue, out, in_, sem):
+        queue.dma_start(out, in_).then_inc(T.sem[sem], 16)
+        incs[sem] = 16
+
+    def product(lhs, rhs, out, n):
+        i = count[0]
+        count[0] += 1
+        bank = T["ps%d" % (i % NBANK)]
+        twait(lhs[1])
+        twait(rhs[1])
+        if i >= NBANK:
+            twait("v%d" % (i - NBANK))
+        g.tensor.matmul(bank[:, 0:n], lhs[0], rhs[0], start=True, stop=True).then_inc(T.sem["t%d" % i], 1)
+        incs["t%d" % i] = 1
+        wait(g.vector, "t%d" % i)
+        g.vector.tensor_copy(out, bank[:, 0:n]).then_inc(T.sem["v%d" % i], 1)
+        incs["v%d" % i] = 1
+        return (out, "v%d" % i)
+
+    def newslot(n):
+        s = count[1]
+        count[1] += 1
+        return T.prod[:, s * P:s * P + n]
+
+    def fire(label, src):
+        trs = []
+        for (dsts, mask, sem, buf, c0, c1) in calls.get((core, label), []):
+            ids = []
+            for d in dsts:
+                rid, pid = topo.addr(d, core)
+                ids.append(DstId(rid=rid, pnc=pid))
+            s = src if src is not None else T[buf][:, c0:c1]
+            if label in ("scatter", "scatter2", "full"):
+                s = T.yout[:, c0:c1]
+            trs.append(RemoteDMATransfer(dst_ids=ids, dma_engine_mask=mask, remote_sem=T.sem[sem], srcs=[s],
+                                         dsts=[T[buf][:, c0:c1] for d in dsts]))
+            incs["sent"] = incs.get("sent", 0) + bits(mask)
+        if trs:
+            g.remote_dma_fused(trs, local_sem=T.sem.sent)
+
+    def finish():
+        for sem in sorted(incs):
+            if sem not in waited:
+                wait(g, sem)
+
+    if core == L["root"]:
+        load(g.sync, T.xin[:, :], T.x[:, :], "ldx")
+        load(g.scalar, T.own2[:, :], T.m[:, :], "ldb")
+        done = [product((T.own2[:, :], "ldb"), (T.xin[:, q * w:(q + 1) * w], "ldx"), T.yout[:, q * w:(q + 1) * w], w)
+                for q in range(nq)]
+        for d in done:
+            wait(g, d[1])
+        fire("scatter", None)
+        fire("scatter2", None)
+        fire("full", None)
+        wait(g.sync, "sent")
+        load(g.sync, T.y[:, :], T.yout[:, :], "st0")
+        finish()
+        return
+
+    n1, n2, leaves, given, final, urgent = L["work"][core]
+    chipcores = L["A"] if core in L["A"] else L["B"]
+    have = {}
+    mine = L["given_away"](core)
+    s = L["slot"][core]
+    load(g.sync, T.lf[:, s * P:(s + 1) * P], T.mt[:, :] if mine[2] else T.m[:, :], "lda")
+    have[mine] = (T.lf[:, s * P:(s + 1) * P], "lda")
+    other = (rank, rank, not mine[2])
+    if other in leaves:
+        load(g.scalar, T.own2[:, :], T.mt[:, :] if other[2] else T.m[:, :], "ldb")
+        have[other] = (T.own2[:, :], "ldb")
+    for c in chipcores:
+        lfc = L["given_away"](c) if c != L["root"] else None
+        if c != core and lfc in leaves:
+            sc = L["slot"][c]
+            have[lfc] = (T.lf[:, sc * P:(sc + 1) * P], "lf%d" % sc)
+    for nd in given:
+        have[nd] = (T.hp[:, :], "hp")
+
+    def make(nd):
+        a, b, tr = nd
+        t = split(a, b)
+        left, right = have[(a, t - 1, True)], have[(t, b, False)]
+        have[nd] = product(right, left, newslot(P), P) if tr else product(left, right, newslot(P), P)
+
+    if (core, "leaf1") in calls or (core, "leaf2") in calls:
+        wait(g, "lda")
+        fire("leaf1", None)
+        fire("leaf2", None)
+
+    for nd in n1:
+        make(nd)
+    q0 = L["piece"].get(core)
+    if core in L["relays"]:
+        p7 = product(have[urgent[0]], (T.pl[:, q0 * w:(q0 + 1) * w], "pq%d" % q0), newslot(w), w)
+        wait(g, p7[1])
+        fire("p7", p7[0])
+    if core == L["helper"]:
+        wait(g, have[L["shared"]][1])
+        fire("node", have[L["shared"]][0])
+    if (core, "fwd") in calls:
+        wait(g, "pq%d" % q0)
+        fire("fwd", None)
+    for nd in n2:
+        make(nd)
+
+    whole = core in L["home"]
+    qs = list(range(nq)) if whole else [(q0 + k) % nq for k in range(nq)]
+    for k, q in enumerate(qs):
+        rhs = (T.pf[:, q * w:(q + 1) * w], "pf") if whole else (T.pl[:, q * w:(q + 1) * w], "pq%d" % q)
+        res = product(have[final], rhs, T.yout[:, q * w:(q + 1) * w], w)
+        queue = g.sync if k % 2 == 0 else g.scalar
+        wait(queue, res[1])
+        load(queue, T.y[:, q * w:(q + 1) * w], res[0], "st%d" % k)
+    finish()

@@ -11,6 +11,7 @@ SCRATCH = {
     "lf": ("sbuf", [P, 8 * P], "bfloat16"),
     "own2": ("sbuf", [P, P], "bfloat16"),
     "hp": ("sbuf", [P, P], "bfloat16"),
+    "sa": ("sbuf", [P, P], "bfloat16"),
     "prod": ("sbuf", [P, NSLOT * P], "bfloat16"),
     "pl": ("sbuf", [P, F], "bfloat16"),
     "pf": ("sbuf", [P, F], "bfloat16"),
@@ -19,8 +20,9 @@ SCRATCH = {
 for _b in range(NBANK):
     SCRATCH["ps%d" % _b] = ("psum", [P, 512], "float32")
 
-SEMAPHORES = (["lda", "ldb", "ldx", "pf", "hp", "sent"] + ["lf%d" % i for i in range(8)] + ["pq%d" % i for i in range(4)]
-              + ["st%d" % i for i in range(4)] + ["t%d" % i for i in range(NPROD)] + ["v%d" % i for i in range(NPROD)])
+SEMAPHORES = (["lda", "ldb", "ldx", "pf", "hp", "sa", "sent"] + ["lf%d" % i for i in range(8)]
+              + ["pq%d" % i for i in range(4)] + ["st%d" % i for i in range(4)]
+              + ["t%d" % i for i in range(NPROD)] + ["v%d" % i for i in range(NPROD)])
 
 
 def bits(m):
@@ -96,6 +98,11 @@ def layout(cores, topo):
     for grp in (b1, b2):
         for k, c in enumerate(grp):
             piece[c] = k
+    holders = []
+    for q, c in enumerate(relays):
+        h = [d for d in B if topo.die(d) == topo.die(c) and d not in holders][0]
+        holders.append(h)
+        piece[h] = q
     helper = B[-1]
     shared = (rk[b1[0]], rk[b1[-1]], True)
     first = {}
@@ -103,6 +110,7 @@ def layout(cores, topo):
         first[c] = rk[A[1]]
     for c in B:
         first[c] = rk[B[0]]
+    chipa = (rk[A[1]], rk[A[-1]], True)
 
     def given_away(c):
         j = rk[c]
@@ -111,7 +119,7 @@ def layout(cores, topo):
     work = {}
     for c in cores[1:]:
         given = [shared] if (c in b2 and c != helper) else []
-        urgent = [(first[c], rk[A[-1]], False)] if c in relays else ([shared] if c == helper else [])
+        urgent = [chipa] if c in relays else ([shared] if c == helper else [])
         final = (first[c], rk[c], False)
         n1, n2, leaves = [], [], []
         for nd in urgent:
@@ -152,15 +160,19 @@ def layout(cores, topo):
             for label, dsts in (("leaf1", [c for c in need if c in prio]), ("leaf2", [c for c in need if c not in prio])):
                 if dsts:
                     add(src, label, dsts, topo.mask(src, dsts[0]), "lf%d" % s, "lf", s * P, (s + 1) * P)
-    for c in relays:
+    for q, c in enumerate(relays):
+        add(c, "cross", [holders[q]], topo.mask(c, holders[q]), "pq%d" % q, "pl", q * w, (q + 1) * w)
+    for c in far:
         q = piece[c]
-        dsts = [d for d in B if piece[d] == q]
-        add(c, "p7", dsts, topo.mask(c, dsts[0]), "pq%d" % q, "pl", q * w, (q + 1) * w)
-    for chipcores, holders in ((A, far), (B, B)):
-        for c in holders:
-            q = piece[c]
-            dsts = neighbours(c, chipcores)
-            add(c, "fwd", dsts, topo.mask(c, dsts[0]), "pq%d" % q, "pl", q * w, (q + 1) * w)
+        dsts = neighbours(c, A)
+        add(c, "fwd", dsts, topo.mask(c, dsts[0]), "pq%d" % q, "pl", q * w, (q + 1) * w)
+    for q, c in enumerate(holders):
+        dsts = [d for d in B if d != c]
+        add(c, "fwd", dsts, topo.mask(c, dsts[0]), "pq%d" % q, "pl", q * w, (q + 1) * w)
+    for c in relays:
+        team = [d for d in relays if topo.die(d) == topo.die(c)]
+        dsts = [d for d in B if topo.die(d) == topo.die(c)][team.index(c)::len(team)]
+        add(c, "chipa", dsts, topo.mask(c, dsts[0]), "sa", "sa", 0, P)
     dsts = [c for c in b2 if c != helper]
     add(helper, "node", dsts, topo.mask(helper, dsts[0]), "hp", "hp", 0, P)
 
@@ -290,24 +302,27 @@ def rank_program(g, core, T, topo):
     for nd in n1:
         make(nd)
     q0 = L["piece"].get(core)
-    if core in L["relays"]:
-        p7 = product(have[urgent[0]], (T.pl[:, q0 * w:(q0 + 1) * w], "pq%d" % q0), newslot(w), w)
-        wait(g, p7[1])
-        fire("p7", p7[0])
     if core == L["helper"]:
         wait(g, have[L["shared"]][1])
         fire("node", have[L["shared"]][0])
-    if (core, "fwd") in calls:
+    if (core, "cross") in calls or (core, "fwd") in calls:
         wait(g, "pq%d" % q0)
+        fire("cross", None)
         fire("fwd", None)
+    if core in L["relays"]:
+        wait(g, have[urgent[0]][1])
+        fire("chipa", have[urgent[0]][0])
     for nd in n2:
         make(nd)
+    mat = have[final]
+    if core in L["B"]:
+        mat = product((T.sa[:, :], "sa"), mat, newslot(P), P)
 
     whole = core in L["home"]
     qs = list(range(nq)) if whole else [(q0 + k) % nq for k in range(nq)]
     for k, q in enumerate(qs):
         rhs = (T.pf[:, q * w:(q + 1) * w], "pf") if whole else (T.pl[:, q * w:(q + 1) * w], "pq%d" % q)
-        res = product(have[final], rhs, T.yout[:, q * w:(q + 1) * w], w)
+        res = product(mat, rhs, T.yout[:, q * w:(q + 1) * w], w)
         queue = g.sync if k % 2 == 0 else g.scalar
         wait(queue, res[1])
         load(queue, T.y[:, q * w:(q + 1) * w], res[0], "st%d" % k)

from concourse.bass import DstId, RemoteDMATransfer

P = 128
F = 512
NBANK = 8
NSLOT = 10
NPROD = 14

SCRATCH = {
    "xin": ("sbuf", [P, F], "bfloat16"),
    "lf": ("sbuf", [P, 8 * P], "bfloat16"),
    "own2": ("sbuf", [P, P], "bfloat16"),
    "hp": ("sbuf", [P, P], "bfloat16"),
    "sa": ("sbuf", [P, P], "bfloat16"),
    "prod": ("sbuf", [P, NSLOT * P], "bfloat16"),
    "pl": ("sbuf", [P, F], "bfloat16"),
    "pf": ("sbuf", [P, F], "bfloat16"),
    "yout": ("sbuf", [P, F], "bfloat16"),
}
for _b in range(NBANK):
    SCRATCH["ps%d" % _b] = ("psum", [P, 512], "float32")

SEMAPHORES = (["lda", "ldb", "ldx", "pf", "hp", "sa", "sent"] + ["lf%d" % i for i in range(8)]
              + ["pq%d" % i for i in range(4)] + ["st%d" % i for i in range(4)]
              + ["t%d" % i for i in range(NPROD)] + ["v%d" % i for i in range(NPROD)])


def bits(m):
    return bin(m).count("1")


def share(m, k, n):
    es = [e for e in range(m.bit_length()) if (m >> e) & 1]
    out = 0
    for e in es[k::n]:
        out |= 1 << e
    return out


def split(a, b):
    k = b.bit_length()
    while True:
        t = (b >> k) << k
        if t > a:
            return t
        k -= 1


def expand(node, given, nodes, leaves):
    a, b, tr = node
    if node in given or node in nodes or node in leaves:
        return
    if a == b:
        leaves.append(node)
        return
    t = split(a, b)
    expand((a, t - 1, True), given, nodes, leaves)
    expand((t, b, False), given, nodes, leaves)
    nodes.append(node)


def height(node, given):
    a, b, tr = node
    if a == b or node in given:
        return 0
    t = split(a, b)
    return 1 + max(height((a, t - 1, True), given), height((t, b, False), given))


def layout(cores, topo):
    root = cores[0]
    rk = {}
    for i, c in enumerate(cores):
        rk[c] = i

    def place(c):
        return (topo.host(c), topo.chip(c))

    def neighbours(c, chipcores):
        return [d for d in chipcores if d != c and topo.die(d) == topo.die(c)]

    A = [c for c in cores if place(c) == place(root)]
    B = [c for c in cores if place(c) != place(root)]
    relays = [c for c in A if c != root and topo.may_write(c, B[0])]
    nq = len(relays)
    w = F // nq
    home = neighbours(root, A)
    far = [c for c in A if topo.die(c) != topo.die(root)]
    piece = {}
    for q, c in enumerate(relays):
        piece[c] = q
    spare = [q for q, c in enumerate(relays) if c not in far]
    for c in far:
        if c not in piece:
            piece[c] = spare.pop(0)
    b1 = [c for c in B if topo.die(c) == topo.die(B[0])]
    b2 = [c for c in B if topo.die(c) != topo.die(B[0])]
    for grp in (b1, b2):
        for k, c in enumerate(grp):
            piece[c] = k
    holders = []
    for q, c in enumerate(relays):
        h = [d for d in B if topo.die(d) == topo.die(c) and d not in holders][0]
        holders.append(h)
        piece[h] = q
    helper = B[-1]
    shared = (rk[b1[0]], rk[b1[-1]], True)
    first = {}
    for c in A:
        first[c] = rk[A[1]]
    for c in B:
        first[c] = rk[B[0]]
    chipa = (rk[A[1]], rk[A[-1]], True)

    def given_away(c):
        j = rk[c]
        return (j, j, j % 2 == 0 or j == first[c])

    work = {}
    for c in cores[1:]:
        given = [shared] if (c in b2 and c != helper) else []
        urgent = [chipa] if c in relays else ([shared] if c == helper else [])
        final = (first[c], rk[c], False)
        n1, n2, leaves = [], [], []
        for nd in urgent:
            expand(nd, given, n1, leaves)
        n2 = list(n1)
        expand(final, given, n2, leaves)
        n2 = n2[len(n1):]
        n1.sort(key=lambda nd: height(nd, given))
        n2.sort(key=lambda nd: height(nd, given))
        work[c] = (n1, n2, leaves, given, final, urgent)

    calls = {}

    def add(src, label, dsts, mask, sem, buf, c0, c1):
        if dsts:
            calls.setdefault((src, label), []).append((dsts, mask, sem, buf, c0, c1))

    hr = [c for c in relays if c in home]
    fr = [c for c in relays if c in far]
    order = []
    for i in range(max(len(hr), len(fr))):
        order += hr[i:i + 1] + fr[i:i + 1]
    for k, c in enumerate(order):
        q = piece[c]
        add(root, "scatter", [c], share(topo.mask(root, c), k, len(order)), "pq%d" % q, "pl", q * w, (q + 1) * w)
    rest = [c for c in far if c not in relays]
    for k, c in enumerate(rest):
        q = piece[c]
        add(root, "scatter2", [c], share(topo.mask(root, c), k, len(rest)), "pq%d" % q, "pl", q * w, (q + 1) * w)
    add(root, "full", home, topo.mask(root, home[0]), "pf", "pf", 0, F)
    slot = {}
    for chipcores, prio in ((A, relays), (B, [helper])):
        for s, src in enumerate(chipcores):
            slot[src] = s
            if src == root:
                continue
            need = [c for c in chipcores if c != src and c != root and given_away(src) in work[c][2]]
            for label, dsts in (("leaf1", [c for c in need if c in prio]), ("leaf2", [c for c in need if c not in prio])):
                if dsts:
                    add(src, label, dsts, topo.mask(src, dsts[0]), "lf%d" % s, "lf", s * P, (s + 1) * P)
    for q, c in enumerate(relays):
        add(c, "cross", [holders[q]], topo.mask(c, holders[q]), "pq%d" % q, "pl", q * w, (q + 1) * w)
    for c in far:
        q = piece[c]
        dsts = neighbours(c, A)
        add(c, "fwd", dsts, topo.mask(c, dsts[0]), "pq%d" % q, "pl", q * w, (q + 1) * w)
    for q, c in enumerate(holders):
        dsts = [d for d in B if d != c]
        add(c, "fwd", dsts, topo.mask(c, dsts[0]), "pq%d" % q, "pl", q * w, (q + 1) * w)
    for c in relays:
        team = [d for d in relays if topo.die(d) == topo.die(c)]
        dsts = [d for d in B if topo.die(d) == topo.die(c)][team.index(c)::len(team)]
        add(c, "chipa", dsts, topo.mask(c, dsts[0]), "sa", "sa", 0, P)
    dsts = [c for c in b2 if c != helper]
    add(helper, "node", dsts, topo.mask(helper, dsts[0]), "hp", "hp", 0, P)

    expect = {}
    for key in calls:
        for (dsts, mask, sem, buf, c0, c1) in calls[key]:
            for d in dsts:
                expect[(d, sem)] = expect.get((d, sem), 0) + bits(mask)
    return dict(root=root, rk=rk, A=A, B=B, relays=relays, nq=nq, w=w, home=home, far=far, piece=piece, helper=helper,
                shared=shared, work=work, calls=calls, expect=expect, slot=slot, given_away=given_away)


def rank_program(g, core, T, topo):
    rank = T.rank_of(core)
    if rank is None:
        return
    L = layout(list(T.cores), topo)
    nq, w, calls, expect = L["nq"], L["w"], L["calls"], L["expect"]
    incs = {}
    waited = set()
    tdone = set()
    count = [0, 0]

    for (d, sem) in expect:
        if d == core:
            incs[sem] = expect[(d, sem)]

    def wait(queue, sem):
        queue.wait_ge(T.sem[sem], incs[sem])
        waited.add(sem)

    def twait(sem):
        if sem not in tdone:
            tdone.add(sem)
            wait(g.tensor, sem)

    def load(queue, out, in_, sem):
        queue.dma_start(out, in_).then_inc(T.sem[sem], 16)
        incs[sem] = 16

    def product(lhs, rhs, out, n):
        i = count[0]
        count[0] += 1
        bank = T["ps%d" % (i % NBANK)]
        twait(lhs[1])
        twait(rhs[1])
        if i >= NBANK:
            twait("v%d" % (i - NBANK))
        g.tensor.matmul(bank[:, 0:n], lhs[0], rhs[0], start=True, stop=True).then_inc(T.sem["t%d" % i], 1)
        incs["t%d" % i] = 1
        wait(g.vector, "t%d" % i)
        g.vector.tensor_copy(out, bank[:, 0:n]).then_inc(T.sem["v%d" % i], 1)
        incs["v%d" % i] = 1
        return (out, "v%d" % i)

    def newslot(n):
        s = count[1]
        count[1] += 1
        return T.prod[:, s * P:s * P + n]

    def fire(label, src):
        trs = []
        for (dsts, mask, sem, buf, c0, c1) in calls.get((core, label), []):
            ids = []
            for d in dsts:
                rid, pid = topo.addr(d, core)
                ids.append(DstId(rid=rid, pnc=pid))
            s = src if src is not None else T[buf][:, c0:c1]
            if label in ("scatter", "scatter2", "full"):
                s = T.yout[:, c0:c1]
            trs.append(RemoteDMATransfer(dst_ids=ids, dma_engine_mask=mask, remote_sem=T.sem[sem], srcs=[s],
                                         dsts=[T[buf][:, c0:c1] for d in dsts]))
            incs["sent"] = incs.get("sent", 0) + bits(mask)
        if trs:
            g.remote_dma_fused(trs, local_sem=T.sem.sent)

    def finish():
        for sem in sorted(incs):
            if sem not in waited:
                wait(g, sem)

    if core == L["root"]:
        load(g.sync, T.xin[:, :], T.x[:, :], "ldx")
        load(g.scalar, T.own2[:, :], T.m[:, :], "ldb")
        done = [product((T.own2[:, :], "ldb"), (T.xin[:, q * w:(q + 1) * w], "ldx"), T.yout[:, q * w:(q + 1) * w], w)
                for q in range(nq)]
        for d in done:
            wait(g, d[1])
        fire("scatter", None)
        fire("scatter2", None)
        fire("full", None)
        wait(g.sync, "sent")
        load(g.sync, T.y[:, :], T.yout[:, :], "st0")
        finish()
        return

    n1, n2, leaves, given, final, urgent = L["work"][core]
    chipcores = L["A"] if core in L["A"] else L["B"]
    have = {}
    mine = L["given_away"](core)
    s = L["slot"][core]
    load(g.sync, T.lf[:, s * P:(s + 1) * P], T.mt[:, :] if mine[2] else T.m[:, :], "lda")
    have[mine] = (T.lf[:, s * P:(s + 1) * P], "lda")
    other = (rank, rank, not mine[2])
    if other in leaves:
        load(g.scalar, T.own2[:, :], T.mt[:, :] if other[2] else T.m[:, :], "ldb")
        have[other] = (T.own2[:, :], "ldb")
    for c in chipcores:
        lfc = L["given_away"](c) if c != L["root"] else None
        if c != core and lfc in leaves:
            sc = L["slot"][c]
            have[lfc] = (T.lf[:, sc * P:(sc + 1) * P], "lf%d" % sc)
    for nd in given:
        have[nd] = (T.hp[:, :], "hp")

    def make(nd):
        a, b, tr = nd
        t = split(a, b)
        left, right = have[(a, t - 1, True)], have[(t, b, False)]
        have[nd] = product(right, left, newslot(P), P) if tr else product(left, right, newslot(P), P)

    if (core, "leaf1") in calls or (core, "leaf2") in calls:
        wait(g, "lda")
        fire("leaf1", None)
        fire("leaf2", None)

    for nd in n1:
        make(nd)
    q0 = L["piece"].get(core)
    if core == L["helper"]:
        wait(g, have[L["shared"]][1])
        fire("node", have[L["shared"]][0])
    if (core, "cross") in calls or (core, "fwd") in calls:
        wait(g, "pq%d" % q0)
        fire("cross", None)
        fire("fwd", None)
    if core in L["relays"]:
        wait(g, have[urgent[0]][1])
        fire("chipa", have[urgent[0]][0])
    for nd in n2:
        make(nd)
    mat = have[final]
    if core in L["B"]:
        mat = product((T.sa[:, :], "sa"), mat, newslot(P), P)

    whole = core in L["home"]
    qs = list(range(nq)) if whole else [(q0 + k) % nq for k in range(nq)]
    for k, q in enumerate(qs):
        rhs = (T.pf[:, q * w:(q + 1) * w], "pf") if whole else (T.pl[:, q * w:(q + 1) * w], "pq%d" % q)
        res = product(mat, rhs, T.yout[:, q * w:(q + 1) * w], w)
        queue = g.sync if k % 2 == 0 else g.scalar
        wait(queue, res[1])
        load(queue, T.y[:, q * w:(q + 1) * w], res[0], "st%d" % k)
    finish()
